import numpy as np
import ml_dtypes


def mxq(x, axis, fmt="e4m3"):
    dtype, down = {"e4m3": (ml_dtypes.float8_e4m3fn, 7), "e5m2": (ml_dtypes.float8_e5m2, 14)}[fmt]
    v = np.moveaxis(np.asarray(x, np.float32).astype(ml_dtypes.bfloat16).astype(np.float64), axis, -1)
    blocks = v.reshape(v.shape[:-1] + (-1, 32))
    amax = np.abs(blocks).max(-1, keepdims=True)
    byte = np.maximum(np.where(amax > 0, np.frexp(amax)[1] - 1 + 127, 0) - down, 1)
    scale = np.exp2(byte - 127.0)
    codes = (blocks / scale).astype(np.float32).astype(dtype).astype(np.float64)
    return np.moveaxis((codes * scale).reshape(v.shape), -1, axis)


WIDE = False


def mx_kscale(k):
    if not WIDE:
        return np.ones(k)
    levels = np.array([30, -30])
    if k % 512:
        return np.exp2(np.random.permutation(np.resize(levels, k // 32))).repeat(32)
    a = np.empty((k // 512, 16))
    for p in range(k // 512):
        a[p, :8] = np.random.permutation(np.resize(levels, 8))
        for g in range(8):
            far = levels[np.abs(levels - a[p, g]) >= 10]
            a[p, g + 8] = far[np.random.randint(len(far))]
    return np.exp2(a.ravel()).repeat(32)


def f64(x):
    return np.asarray(x).astype(np.float64)


def striped(idx):
    return np.tile(idx.reshape(-1, 16).T, (8, 1)).astype(np.uint16)


def unstriped(offs):
    return offs[:16].T.reshape(-1).astype(np.int64)


def d_relu2(v):
    return 2.0 * np.maximum(v, 0.0)


K, T, E, C, H, N = 128, 1280, 2, 512, 512, 512


def by_expert(wq, xq):
    return np.concatenate([wq[e].T @ xq[:, e * C:(e + 1) * C] for e in range(E)], axis=1)


def setup_inputs():
    n = np.random.standard_normal
    slot_token = np.random.permutation(T)[:E * C]
    s = mx_kscale(N)[:, None]
    z = np.ones(T); z[slot_token] = mx_kscale(E * C)
    return {
        "xT": (n((K, T)) * z[None, :]).astype(np.float32),
        "dyT": (n((N, T)) * s).astype(np.float32),
        "a": n((H, E * C)).astype(np.float32),
        "w2": (n((E, N, H)) / np.sqrt(N) / s[None]).astype(np.float32),
        "gate": np.tile(np.random.uniform(0.2, 1.0, E * C) / z[slot_token], (N, 1)).astype(np.float32),
        "offs": striped(slot_token),
    }


def reference(xT, dyT, a, w2, gate, offs):
    idx = unstriped(offs)
    gq = mxq(f64(gate) * f64(dyT)[:, idx], 0, "e5m2")
    dh = by_expert(mxq(f64(w2), 1, "e4m3"), gq)
    da = mxq(dh * d_relu2(f64(a)), 1, "e5m2")
    xq = mxq(f64(xT)[:, idx], 1, "e4m3")
    return np.stack([(xq[:, e * C:(e + 1) * C] @ da[:, e * C:(e + 1) * C].T) for e in range(E)])

@@ -1,0 +1,133 @@
+from contextlib import ExitStack
+
+import concourse.mybir as mybir
+from concourse.masks import make_identity
+
+K, T, E, C, H, N = 128, 1280, 2, 512, 512, 512
+P = 128
+FLOPS = 2 * E * C * H * (N + K)
+BYTES = 4 * (K * T + N * T + H * E * C + E * N * H + E * C + E * K * H) + 2 * P * (E * C // 16)
+
+F32 = mybir.dt.float32
+BF16 = mybir.dt.bfloat16
+U32 = mybir.dt.uint32
+U16 = mybir.dt.uint16
+U8 = mybir.dt.uint8
+E4 = mybir.dt.float8_e4m3fn_x4
+E5 = mybir.dt.float8_e5m2_x4
+ALU = mybir.AluOpType
+COPY = mybir.ActivationFunctionType.Copy
+
+
+def tile_moe_mlp_relu2_kernel(tc, xT, dyT, a, w2, gate, offs, out):
+    nc = tc.nc
+    with ExitStack() as ctx:
+        sb = ctx.enter_context(tc.tile_pool(name="sb", bufs=1))
+        ps = ctx.enter_context(tc.psum_pool(name="ps", bufs=1))
+
+        def tile(name, shape, dtype):
+            return sb.tile(shape, dtype, name=name, align_bytes=64)
+
+        offsets = sb.tile([P, E * C // 16], U16, name="offsets")
+        nc.sync.dma_start(offsets[:], offs)
+        lists = [offsets[:, e * (C // 16) : (e + 1) * (C // 16)] for e in range(E)]
+
+        dy_rows = dyT.rearrange("(p t) w -> p t w", t=4)
+        dy = [tile(f"dy{t}", [P, T], F32) for t in range(4)]
+        x32 = tile("x32", [P, T], F32)
+        gate_sb = tile("gate_sb", [P, E * C], F32)
+        w_raw = [tile(f"w_raw{e}", [P, 4, H], F32) for e in range(E)]
+        a_sb = [[tile(f"a{e}{b}", [P, C], F32) for b in range(4)] for e in range(E)]
+
+        nc.sync.dma_start(dy[0][:], dy_rows[:, 0, :])
+        nc.sync.dma_start(dy[1][:], dy_rows[:, 1, :])
+        nc.sync.dma_start(x32[:], xT)
+        nc.sync.dma_start(dy[2][:], dy_rows[:, 2, :])
+        nc.sync.dma_start(dy[3][:], dy_rows[:, 3, :])
+        nc.sync.dma_start(gate_sb[:], gate[0:P, :])
+        for e in range(E):
+            nc.sync.dma_start(w_raw[e][:], w2[e].rearrange("(p t) i -> p t i", t=4))
+            for b in range(4):
+                nc.sync.dma_start(a_sb[e][b][:], a[b * P : (b + 1) * P, e * C : (e + 1) * C])
+
+        ident = tile("ident", [P, P], F32)
+        make_identity(nc, ident[:])
+
+        x16 = tile("x16", [P, T], BF16)
+        nc.scalar.copy(x16[:], x32[:])
+        x_bank = ps.tile([P, E, 2, P], F32, name="x_bank", tag="xo")
+        for e in range(E):
+            xg = tile(f"xg{e}", [P, C], BF16)
+            nc.scalar.activation(xg[:], x16[:].indirect(lists[e]), COPY)
+            words = xg[:].bitcast(F32)
+            for u in range(2):
+                nc.tensor.transpose(x_bank[:, e, u, :], words[:, u : C // 2 : 2], ident[:])
+        x_in = tile("x_in", [P, E * K * 4], BF16)
+        nc.scalar.copy(
+            x_in[:].bitcast(F32).rearrange("p (e k u) -> p e k u", e=E, u=2),
+            x_bank[:].rearrange("p e u k -> p e k u"),
+        )
+        x_codes = tile("x_codes", [P, E * K], U32)
+        x_scales = tile("x_scales", [P, E * K], U8)
+        nc.vector.quantize_mx(x_codes[:].bitcast(E4), x_scales[:], x_in[:])
+
+        g32 = [tile(f"g32_{e}", [P, 4, C], F32) for e in range(E)]
+        for t in range(3):
+            for e in range(E):
+                nc.vector.tensor_copy(g32[e][:, t, :], dy[t][:].indirect(lists[e]))
+
+        for e in range(E):
+            nc.vector.tensor_copy(g32[e][:, 3, :], dy[3][:].indirect(lists[e]))
+            g_in = tile(f"g_in{e}", [P, C * 4], BF16)
+            nc.vector.tensor_tensor(
+                g_in[:].rearrange("p (c i t) -> p c t i", i=4, t=4),
+                g32[e][:].rearrange("p t (c i) -> p c t i", i=4),
+                gate_sb[:, e * C : (e + 1) * C].rearrange("p (c i) -> p c i", i=4).unsqueeze(2).to_broadcast([P, C // 4, 4, 4]),
+                ALU.mult,
+            )
+            w_in = tile(f"w_in{e}", [P, H * 4], BF16)
+            nc.scalar.copy(
+                w_in[:].rearrange("p (c i t) -> p c t i", i=4, t=4),
+                w_raw[e][:].rearrange("p t (c i) -> p c t i", i=4),
+            )
+            w_codes = tile(f"w_codes{e}", [P, H], U32)
+            w_scales = tile(f"w_scales{e}", [P, H], U8)
+            nc.vector.quantize_mx(w_codes[:].bitcast(E4), w_scales[:], w_in[:])
+            g_codes = tile(f"g_codes{e}", [P, C], U32)
+            g_scales = tile(f"g_scales{e}", [P, C], U8)
+            nc.vector.quantize_mx(g_codes[:].bitcast(E5), g_scales[:], g_in[:])
+
+            da_in = tile(f"da_in{e}", [P, H * 4], BF16)
+            da_codes = tile(f"da_codes{e}", [P, H], U32)
+            da_scales = tile(f"da_scales{e}", [P, H], U8)
+            for pair in range(2):
+                da_bank = ps.tile([P, 2, 2, P], F32, name=f"da_bank{pair}")
+                for j in range(2):
+                    b = 2 * pair + j
+                    cols = slice(b * P, (b + 1) * P)
+                    dh = ps.tile([P, C], F32, name=f"dh{b}")
+                    nc.tensor.matmul_mx(
+                        dh[:], w_codes[:, cols].bitcast(E4), w_scales[:, cols], g_codes[:].bitcast(E5), g_scales[:],
+                        start=True, stop=True,
+                    )
+                    da = tile(f"da{e}{b}", [P, C], BF16)
+                    nc.vector.scalar_tensor_tensor(da[:], a_sb[e][b][:], 0.0, dh[:], ALU.max, ALU.mult)
+                    words = da[:].bitcast(F32)
+                    for u in range(2):
+                        nc.tensor.transpose(da_bank[:, j, u, :], words[:, u : C // 2 : 2], ident[:])
+                half = slice(pair * 1024, (pair + 1) * 1024)
+                nc.scalar.copy(
+                    da_in[:, half].bitcast(F32).rearrange("p (j i u) -> p j i u", j=2, u=2),
+                    da_bank[:].rearrange("p j u i -> p j i u"),
+                )
+                hc = slice(pair * 256, (pair + 1) * 256)
+                nc.vector.quantize_mx(da_codes[:, hc].bitcast(E5), da_scales[:, hc], da_in[:, half])
+            acc = ps.tile([P, H], F32, name=f"acc{e}", tag="xo" if e == 0 else "acc1")
+            kc = slice(e * K, (e + 1) * K)
+            nc.tensor.matmul_mx(
+                acc[:], x_codes[:, kc].bitcast(E4), x_scales[:, kc], da_codes[:].bitcast(E5), da_scales[:],
+                start=True, stop=True,
+            )
+            res = tile(f"res{e}", [P, H], F32)
+            nc.scalar.activation(res[:], acc[:], COPY, scale=2.0)
+            nc.sync.dma_start(out[e], res[:])

@@ -25,109 +25,177 @@ def tile_moe_mlp_relu2_kernel(tc, xT, dyT, a, w2, gate, offs, out):
         sb = ctx.enter_context(tc.tile_pool(name="sb", bufs=1))
         ps = ctx.enter_context(tc.psum_pool(name="ps", bufs=1))
 
-        def tile(name, shape, dtype):
-            return sb.tile(shape, dtype, name=name, align_bytes=64)
+        def tile(name, shape, dtype, tag=None):
+            return sb.tile(shape, dtype, name=name, tag=tag or name, align_bytes=64)
 
+        def bank(name, shape, number):
+            return ps.tile(shape, F32, name=name, tag=f"bank{number}")
+
+        def weave(copy, dst, src):
+            copy(dst.rearrange("p (c i t) -> p c t i", i=4, t=4), src.rearrange("p t (c i) -> p c t i", i=4))
+
+        def quant(codes, scales, src, fmt, first, count):
+            cols = slice(first, first + count)
+            nc.vector.quantize_mx(codes[:, cols].bitcast(fmt), scales[:, cols], src[:, 4 * first : 4 * (first + count)])
+
+        gate_col = tile("gate_col", [P, E, 4], F32)
+        nc.sync.dma_start(gate_col[:], gate[0, :].rearrange("(e n m) -> n e m", e=E, m=4))
         offsets = sb.tile([P, E * C // 16], U16, name="offsets")
         nc.sync.dma_start(offsets[:], offs)
-        lists = [offsets[:, e * (C // 16) : (e + 1) * (C // 16)] for e in range(E)]
+
+        def entries(first, count):
+            return offsets[:, first // 16 : (first + count) // 16]
 
         dy_rows = dyT.rearrange("(p t) w -> p t w", t=4)
         dy = [tile(f"dy{t}", [P, T], F32) for t in range(4)]
         x32 = tile("x32", [P, T], F32)
-        gate_sb = tile("gate_sb", [P, E * C], F32)
-        w_raw = [tile(f"w_raw{e}", [P, 4, H], F32) for e in range(E)]
+        w_raw = [[tile(f"w_raw{e}{h}", [P, 4, H // 2], F32) for h in range(2)] for e in range(E)]
         a_sb = [[tile(f"a{e}{b}", [P, C], F32) for b in range(4)] for e in range(E)]
 
+        def load_w(e, h):
+            nc.sync.dma_start(w_raw[e][h][:], w2[e].rearrange("(p t) i -> p t i", t=4)[:, :, h * 256 : (h + 1) * 256])
+
         nc.sync.dma_start(dy[0][:], dy_rows[:, 0, :])
-        nc.sync.dma_start(dy[1][:], dy_rows[:, 1, :])
         nc.sync.dma_start(x32[:], xT)
+        nc.sync.dma_start(dy[1][:], dy_rows[:, 1, :])
+        load_w(0, 0)
         nc.sync.dma_start(dy[2][:], dy_rows[:, 2, :])
+        load_w(0, 1)
         nc.sync.dma_start(dy[3][:], dy_rows[:, 3, :])
-        nc.sync.dma_start(gate_sb[:], gate[0:P, :])
+        load_w(1, 0)
+        load_w(1, 1)
         for e in range(E):
-            nc.sync.dma_start(w_raw[e][:], w2[e].rearrange("(p t) i -> p t i", t=4))
             for b in range(4):
                 nc.sync.dma_start(a_sb[e][b][:], a[b * P : (b + 1) * P, e * C : (e + 1) * C])
 
         ident = tile("ident", [P, P], F32)
         make_identity(nc, ident[:])
 
-        x16 = tile("x16", [P, T], BF16)
+        gates = tile("gates", [P, E * C], F32)
+        for e in range(E):
+            spread = bank(f"spread{e}", [P, 4, P], e)
+            for m in range(4):
+                nc.tensor.transpose(spread[:, m, :], gate_col[:, e, m : m + 1].to_broadcast([P, P]), ident[:])
+            nc.scalar.copy(
+                gates[:, e * C : (e + 1) * C].rearrange("p (n m) -> p n m", m=4), spread[:].rearrange("p m n -> p n m")
+            )
+
+        x16 = tile("x16", [P, T], BF16, tag="gate_col")
         nc.scalar.copy(x16[:], x32[:])
-        x_bank = ps.tile([P, E, 2, P], F32, name="x_bank", tag="xo")
+        x_bank = bank("x_bank", [P, E, 2, P], 2)
         for e in range(E):
             xg = tile(f"xg{e}", [P, C], BF16)
-            nc.scalar.activation(xg[:], x16[:].indirect(lists[e]), COPY)
+            nc.scalar.activation(xg[:], x16[:].indirect(entries(e * C, C)), COPY)
             words = xg[:].bitcast(F32)
             for u in range(2):
                 nc.tensor.transpose(x_bank[:, e, u, :], words[:, u : C // 2 : 2], ident[:])
+
+        g32 = tile("g32", [P, 4, E * C], F32)
+
+        def gather(t, first, count):
+            cols = slice(first, first + count)
+            nc.vector.tensor_tensor(g32[:, t, cols], dy[t][:].indirect(entries(first, count)), gates[:, cols], ALU.mult)
+
+        gather(0, 0, C)
+        gather(0, C, C)
+        gather(1, 0, E * C)
+        gather(2, 0, E * C)
+        gather(3, 0, C // 2)
+        gather(3, C // 2, C // 2)
+        gather(3, C, C)
+
+        g_in = [tile(f"g_in{e}", [P, C * 4], BF16) for e in range(E)]
+        g_codes = [tile(f"g_codes{e}", [P, C], U32) for e in range(E)]
+        g_scales = [tile(f"g_scales{e}", [P, C], U8) for e in range(E)]
+        w_in = [tile("w_in0", [P, H * 4], BF16, tag="x32"), tile("w_in1", [P, H * 4], BF16, tag="dy3")]
+        w_codes = [tile("w_codes0", [P, H], U32, tag="gates"), tile("w_codes1", [P, H], U32)]
+        w_scales = [tile(f"w_scales{e}", [P, H], U8) for e in range(E)]
         x_in = tile("x_in", [P, E * K * 4], BF16)
+        x_codes = tile("x_codes", [P, E * K], U32)
+        x_scales = tile("x_scales", [P, E * K], U8, tag="w_raw01")
+
+        def weave_g(e, h, copy):
+            weave(copy, g_in[e][:, h * 1024 : (h + 1) * 1024], g32[:, :, e * C + h * 256 : e * C + (h + 1) * 256])
+
+        def weave_w(e, h):
+            weave(nc.scalar.copy, w_in[e][:, h * 1024 : (h + 1) * 1024], w_raw[e][h][:])
+
+        weave_w(0, 0)
         nc.scalar.copy(
             x_in[:].bitcast(F32).rearrange("p (e k u) -> p e k u", e=E, u=2),
             x_bank[:].rearrange("p e u k -> p e k u"),
         )
-        x_codes = tile("x_codes", [P, E * K], U32)
-        x_scales = tile("x_scales", [P, E * K], U8)
-        nc.vector.quantize_mx(x_codes[:].bitcast(E4), x_scales[:], x_in[:])
+        weave_w(0, 1)
+        weave_g(0, 0, nc.scalar.copy)
+        weave_g(0, 1, nc.scalar.copy)
+        quant(w_codes[0], w_scales[0], w_in[0], E4, 0, H)
+        weave_g(1, 0, nc.vector.tensor_copy)
+        quant(g_codes[0], g_scales[0], g_in[0], E5, 0, C)
+        quant(x_codes, x_scales, x_in, E4, 0, E * K)
+        weave_g(1, 1, nc.scalar.copy)
+        weave_w(1, 0)
+        weave_w(1, 1)
 
-        g32 = [tile(f"g32_{e}", [P, 4, C], F32) for e in range(E)]
-        for t in range(3):
-            for e in range(E):
-                nc.vector.tensor_copy(g32[e][:, t, :], dy[t][:].indirect(lists[e]))
+        da_in = [tile(f"da_in{e}", [P, H * 4], BF16) for e in range(E)]
+        da_scales = [tile(f"da_scales{e}", [P, H], U8) for e in range(E)]
+        dh = {}
 
-        for e in range(E):
-            nc.vector.tensor_copy(g32[e][:, 3, :], dy[3][:].indirect(lists[e]))
-            g_in = tile(f"g_in{e}", [P, C * 4], BF16)
-            nc.vector.tensor_tensor(
-                g_in[:].rearrange("p (c i t) -> p c t i", i=4, t=4),
-                g32[e][:].rearrange("p t (c i) -> p c t i", i=4),
-                gate_sb[:, e * C : (e + 1) * C].rearrange("p (c i) -> p c i", i=4).unsqueeze(2).to_broadcast([P, C // 4, 4, 4]),
-                ALU.mult,
-            )
-            w_in = tile(f"w_in{e}", [P, H * 4], BF16)
-            nc.scalar.copy(
-                w_in[:].rearrange("p (c i t) -> p c t i", i=4, t=4),
-                w_raw[e][:].rearrange("p t (c i) -> p c t i", i=4),
-            )
-            w_codes = tile(f"w_codes{e}", [P, H], U32)
-            w_scales = tile(f"w_scales{e}", [P, H], U8)
-            nc.vector.quantize_mx(w_codes[:].bitcast(E4), w_scales[:], w_in[:])
-            g_codes = tile(f"g_codes{e}", [P, C], U32)
-            g_scales = tile(f"g_scales{e}", [P, C], U8)
-            nc.vector.quantize_mx(g_codes[:].bitcast(E5), g_scales[:], g_in[:])
-
-            da_in = tile(f"da_in{e}", [P, H * 4], BF16)
-            da_codes = tile(f"da_codes{e}", [P, H], U32)
-            da_scales = tile(f"da_scales{e}", [P, H], U8)
-            for pair in range(2):
-                da_bank = ps.tile([P, 2, 2, P], F32, name=f"da_bank{pair}")
-                for j in range(2):
-                    b = 2 * pair + j
-                    cols = slice(b * P, (b + 1) * P)
-                    dh = ps.tile([P, C], F32, name=f"dh{b}")
-                    nc.tensor.matmul_mx(
-                        dh[:], w_codes[:, cols].bitcast(E4), w_scales[:, cols], g_codes[:].bitcast(E5), g_scales[:],
-                        start=True, stop=True,
-                    )
-                    da = tile(f"da{e}{b}", [P, C], BF16)
-                    nc.vector.scalar_tensor_tensor(da[:], a_sb[e][b][:], 0.0, dh[:], ALU.max, ALU.mult)
-                    words = da[:].bitcast(F32)
-                    for u in range(2):
-                        nc.tensor.transpose(da_bank[:, j, u, :], words[:, u : C // 2 : 2], ident[:])
-                half = slice(pair * 1024, (pair + 1) * 1024)
-                nc.scalar.copy(
-                    da_in[:, half].bitcast(F32).rearrange("p (j i u) -> p j i u", j=2, u=2),
-                    da_bank[:].rearrange("p j u i -> p j i u"),
-                )
-                hc = slice(pair * 256, (pair + 1) * 256)
-                nc.vector.quantize_mx(da_codes[:, hc].bitcast(E5), da_scales[:, hc], da_in[:, half])
-            acc = ps.tile([P, H], F32, name=f"acc{e}", tag="xo" if e == 0 else "acc1")
-            kc = slice(e * K, (e + 1) * K)
+        def product(e, b):
+            cols = slice(b * P, (b + 1) * P)
+            dh[e, b] = bank(f"dh{e}{b}", [P, C], 3 + b)
             nc.tensor.matmul_mx(
-                acc[:], x_codes[:, kc].bitcast(E4), x_scales[:, kc], da_codes[:].bitcast(E5), da_scales[:],
+                dh[e, b][:], w_codes[e][:, cols].bitcast(E4), w_scales[e][:, cols], g_codes[e][:].bitcast(E5), g_scales[e][:],
                 start=True, stop=True,
             )
-            res = tile(f"res{e}", [P, H], F32)
-            nc.scalar.activation(res[:], acc[:], COPY, scale=2.0)
-            nc.sync.dma_start(out[e], res[:])
+
+        def turn(e, blocks, number):
+            turned = bank(f"turned{e}{blocks[0]}", [P, len(blocks), 2, P], number)
+            for j, b in enumerate(blocks):
+                da = tile(f"da{e}{b}", [P, C], BF16)
+                nc.vector.scalar_tensor_tensor(da[:], a_sb[e][b][:], 0.0, dh[e, b][:], ALU.max, ALU.mult)
+                words = da[:].bitcast(F32)
+                for u in range(2):
+                    nc.tensor.transpose(turned[:, j, u, :], words[:, u : C // 2 : 2], ident[:])
+            cols = slice(4 * P * blocks[0], 4 * P * (blocks[-1] + 1))
+            nc.scalar.copy(
+                da_in[e][:, cols].bitcast(F32).rearrange("p (j i u) -> p j i u", j=len(blocks), u=2),
+                turned[:].rearrange("p j u i -> p j i u"),
+            )
+
+        for b in range(4):
+            product(0, b)
+        quant(g_codes[1], g_scales[1], g_in[1], E5, 0, C)
+        turn(0, [0, 1], 0)
+        quant(w_codes[1], w_scales[1], w_in[1], E4, 0, H // 2)
+        product(1, 0)
+        product(1, 1)
+        turn(0, [2, 3], 1)
+        quant(w_codes[1], w_scales[1], w_in[1], E4, H // 2, H // 2)
+        product(1, 2)
+        product(1, 3)
+        turn(1, [0, 1], 0)
+        turn(1, [2], 1)
+        turn(1, [3], 2)
+
+        da_codes = [tile("da_codes0", [P, H], U32, tag="a13"), tile("da_codes1", [P, H], U32)]
+
+        def finish(e, pieces, number):
+            acc = bank(f"acc{e}", [P, H], number)
+            kc = slice(e * K, (e + 1) * K)
+            nc.tensor.matmul_mx(
+                acc[:], x_codes[:, kc].bitcast(E4), x_scales[:, kc], da_codes[e][:].bitcast(E5), da_scales[e][:],
+                start=True, stop=True,
+            )
+            width = H // pieces
+            for s in range(pieces):
+                cols = slice(s * width, (s + 1) * width)
+                res = tile(f"res{e}{s}", [P, width], F32)
+                nc.scalar.activation(res[:], acc[:, cols], COPY, scale=2.0)
+                nc.sync.dma_start(out[e][:, cols], res[:])
+
+        quant(da_codes[0], da_scales[0], da_in[0], E5, 0, H)
+        finish(0, 1, 7)
+        quant(da_codes[1], da_scales[1], da_in[1], E5, 0, 2 * P)
+        quant(da_codes[1], da_scales[1], da_in[1], E5, 2 * P, P)
+        quant(da_codes[1], da_scales[1], da_in[1], E5, 3 * P, P)
+        finish(1, 2, 3)

@@ -38,10 +38,11 @@ def tile_moe_mlp_relu2_kernel(tc, xT, dyT, a, w2, gate, offs, out):
             cols = slice(first, first + count)
             nc.vector.quantize_mx(codes[:, cols].bitcast(fmt), scales[:, cols], src[:, 4 * first : 4 * (first + count)])
 
-        gate_col = tile("gate_col", [P, E, 4], F32)
-        nc.sync.dma_start(gate_col[:], gate[0, :].rearrange("(e n m) -> n e m", e=E, m=4))
+        gate_col = [tile(f"gate_col{e}", [P, 4], F32) for e in range(E)]
         offsets = sb.tile([P, E * C // 16], U16, name="offsets")
-        nc.sync.dma_start(offsets[:], offs)
+
+        def load_gate(e):
+            nc.sync.dma_start(gate_col[e][:], gate[0, e * C : (e + 1) * C].rearrange("(n m) -> n m", m=4))
 
         def entries(first, count):
             return offsets[:, first // 16 : (first + count) // 16]
@@ -49,21 +50,22 @@ def tile_moe_mlp_relu2_kernel(tc, xT, dyT, a, w2, gate, offs, out):
         dy_rows = dyT.rearrange("(p t) w -> p t w", t=4)
         dy = [tile(f"dy{t}", [P, T], F32) for t in range(4)]
         x32 = tile("x32", [P, T], F32)
-        w_raw = [[tile(f"w_raw{e}{h}", [P, 4, H // 2], F32) for h in range(2)] for e in range(E)]
+        w_raw = [tile(f"w_raw{e}", [P, 4, H], F32) for e in range(E)]
         a_sb = [[tile(f"a{e}{b}", [P, C], F32) for b in range(4)] for e in range(E)]
 
-        def load_w(e, h):
-            nc.sync.dma_start(w_raw[e][h][:], w2[e].rearrange("(p t) i -> p t i", t=4)[:, :, h * 256 : (h + 1) * 256])
+        def load_w(e):
+            nc.sync.dma_start(w_raw[e][:], w2[e].rearrange("(p t) i -> p t i", t=4))
 
+        load_gate(0)
         nc.sync.dma_start(dy[0][:], dy_rows[:, 0, :])
+        nc.sync.dma_start(offsets[:], offs)
+        load_gate(1)
         nc.sync.dma_start(x32[:], xT)
         nc.sync.dma_start(dy[1][:], dy_rows[:, 1, :])
-        load_w(0, 0)
         nc.sync.dma_start(dy[2][:], dy_rows[:, 2, :])
-        load_w(0, 1)
+        load_w(0)
         nc.sync.dma_start(dy[3][:], dy_rows[:, 3, :])
-        load_w(1, 0)
-        load_w(1, 1)
+        load_w(1)
         for e in range(E):
             for b in range(4):
                 nc.sync.dma_start(a_sb[e][b][:], a[b * P : (b + 1) * P, e * C : (e + 1) * C])
@@ -75,12 +77,12 @@ def tile_moe_mlp_relu2_kernel(tc, xT, dyT, a, w2, gate, offs, out):
         for e in range(E):
             spread = bank(f"spread{e}", [P, 4, P], e)
             for m in range(4):
-                nc.tensor.transpose(spread[:, m, :], gate_col[:, e, m : m + 1].to_broadcast([P, P]), ident[:])
+                nc.tensor.transpose(spread[:, m, :], gate_col[e][:, m : m + 1].to_broadcast([P, P]), ident[:])
             nc.scalar.copy(
                 gates[:, e * C : (e + 1) * C].rearrange("p (n m) -> p n m", m=4), spread[:].rearrange("p m n -> p n m")
             )
 
-        x16 = tile("x16", [P, T], BF16, tag="gate_col")
+        x16 = tile("x16", [P, T], BF16, tag="gate_col1")
         nc.scalar.copy(x16[:], x32[:])
         x_bank = bank("x_bank", [P, E, 2, P], 2)
         for e in range(E):
@@ -107,24 +109,24 @@ def tile_moe_mlp_relu2_kernel(tc, xT, dyT, a, w2, gate, offs, out):
         g_in = [tile(f"g_in{e}", [P, C * 4], BF16) for e in range(E)]
         g_codes = [tile(f"g_codes{e}", [P, C], U32) for e in range(E)]
         g_scales = [tile(f"g_scales{e}", [P, C], U8) for e in range(E)]
-        w_in = [tile("w_in0", [P, H * 4], BF16, tag="x32"), tile("w_in1", [P, H * 4], BF16, tag="dy3")]
+        w_in = [tile("w_in0", [P, H * 4], BF16, tag="xg1"), tile("w_in1", [P, H * 4], BF16, tag="dy3")]
         w_codes = [tile("w_codes0", [P, H], U32, tag="gates"), tile("w_codes1", [P, H], U32)]
         w_scales = [tile(f"w_scales{e}", [P, H], U8) for e in range(E)]
         x_in = tile("x_in", [P, E * K * 4], BF16)
         x_codes = tile("x_codes", [P, E * K], U32)
-        x_scales = tile("x_scales", [P, E * K], U8, tag="w_raw01")
+        x_scales = tile("x_scales", [P, E * K], U8, tag="w_raw0")
 
         def weave_g(e, h, copy):
             weave(copy, g_in[e][:, h * 1024 : (h + 1) * 1024], g32[:, :, e * C + h * 256 : e * C + (h + 1) * 256])
 
         def weave_w(e, h):
-            weave(nc.scalar.copy, w_in[e][:, h * 1024 : (h + 1) * 1024], w_raw[e][h][:])
+            weave(nc.scalar.copy, w_in[e][:, h * 1024 : (h + 1) * 1024], w_raw[e][:, :, h * 256 : (h + 1) * 256])
 
-        weave_w(0, 0)
         nc.scalar.copy(
             x_in[:].bitcast(F32).rearrange("p (e k u) -> p e k u", e=E, u=2),
             x_bank[:].rearrange("p e u k -> p e k u"),
         )
+        weave_w(0, 0)
         weave_w(0, 1)
         weave_g(0, 0, nc.scalar.copy)
         weave_g(0, 1, nc.scalar.copy)

from contextlib import ExitStack

import concourse.mybir as mybir
from concourse.masks import make_identity

K, T, E, C, H, N = 128, 1280, 2, 512, 512, 512
P = 128
FLOPS = 2 * E * C * H * (N + K)
BYTES = 4 * (K * T + N * T + H * E * C + E * N * H + E * C + E * K * H) + 2 * P * (E * C // 16)

F32 = mybir.dt.float32
BF16 = mybir.dt.bfloat16
U32 = mybir.dt.uint32
U16 = mybir.dt.uint16
U8 = mybir.dt.uint8
E4 = mybir.dt.float8_e4m3fn_x4
E5 = mybir.dt.float8_e5m2_x4
ALU = mybir.AluOpType
COPY = mybir.ActivationFunctionType.Copy


def tile_moe_mlp_relu2_kernel(tc, xT, dyT, a, w2, gate, offs, out):
    nc = tc.nc
    with ExitStack() as ctx:
        sb = ctx.enter_context(tc.tile_pool(name="sb", bufs=1))
        ps = ctx.enter_context(tc.psum_pool(name="ps", bufs=1))

        def tile(name, shape, dtype, tag=None):
            return sb.tile(shape, dtype, name=name, tag=tag or name, align_bytes=64)

        def bank(name, shape, number):
            return ps.tile(shape, F32, name=name, tag=f"bank{number}")

        def weave(copy, dst, src):
            copy(dst.rearrange("p (c i t) -> p c t i", i=4, t=4), src.rearrange("p t (c i) -> p c t i", i=4))

        def quant(codes, scales, src, fmt, first, count):
            cols = slice(first, first + count)
            nc.vector.quantize_mx(codes[:, cols].bitcast(fmt), scales[:, cols], src[:, 4 * first : 4 * (first + count)])

        gate_col = [tile(f"gate_col{e}", [P, 4], F32) for e in range(E)]
        offsets = sb.tile([P, E * C // 16], U16, name="offsets")

        def load_gate(e):
            nc.sync.dma_start(gate_col[e][:], gate[0, e * C : (e + 1) * C].rearrange("(n m) -> n m", m=4))

        def entries(first, count):
            return offsets[:, first // 16 : (first + count) // 16]

        dy_rows = dyT.rearrange("(p t) w -> p t w", t=4)
        dy = [tile(f"dy{t}", [P, T], F32) for t in range(4)]
        x32 = tile("x32", [P, T], F32)
        w_raw = [tile(f"w_raw{e}", [P, 4, H], F32) for e in range(E)]
        a_sb = [[tile(f"a{e}{b}", [P, C], F32) for b in range(4)] for e in range(E)]

        def load_w(e):
            nc.sync.dma_start(w_raw[e][:], w2[e].rearrange("(p t) i -> p t i", t=4))

        load_gate(0)
        nc.sync.dma_start(dy[0][:], dy_rows[:, 0, :])
        nc.sync.dma_start(offsets[:], offs)
        load_gate(1)
        nc.sync.dma_start(x32[:], xT)
        nc.sync.dma_start(dy[1][:], dy_rows[:, 1, :])
        nc.sync.dma_start(dy[2][:], dy_rows[:, 2, :])
        load_w(0)
        nc.sync.dma_start(dy[3][:], dy_rows[:, 3, :])
        load_w(1)
        for e in range(E):
            for b in range(4):
                nc.sync.dma_start(a_sb[e][b][:], a[b * P : (b + 1) * P, e * C : (e + 1) * C])

        ident = tile("ident", [P, P], F32)
        make_identity(nc, ident[:])

        gates = tile("gates", [P, E * C], F32)
        for e in range(E):
            spread = bank(f"spread{e}", [P, 4, P], e)
            for m in range(4):
                nc.tensor.transpose(spread[:, m, :], gate_col[e][:, m : m + 1].to_broadcast([P, P]), ident[:])
            nc.scalar.copy(
                gates[:, e * C : (e + 1) * C].rearrange("p (n m) -> p n m", m=4), spread[:].rearrange("p m n -> p n m")
            )

        x16 = tile("x16", [P, T], BF16, tag="gate_col1")
        nc.scalar.copy(x16[:], x32[:])
        x_bank = bank("x_bank", [P, E, 2, P], 2)
        for e in range(E):
            xg = tile(f"xg{e}", [P, C], BF16)
            nc.scalar.activation(xg[:], x16[:].indirect(entries(e * C, C)), COPY)
            words = xg[:].bitcast(F32)
            for u in range(2):
                nc.tensor.transpose(x_bank[:, e, u, :], words[:, u : C // 2 : 2], ident[:])

        g32 = tile("g32", [P, 4, E * C], F32)

        def gather(t, first, count):
            cols = slice(first, first + count)
            nc.vector.tensor_tensor(g32[:, t, cols], dy[t][:].indirect(entries(first, count)), gates[:, cols], ALU.mult)

        gather(0, 0, C)
        gather(0, C, C)
        gather(1, 0, E * C)
        gather(2, 0, E * C)
        gather(3, 0, C // 2)
        gather(3, C // 2, C // 2)
        gather(3, C, C)

        g_in = [tile(f"g_in{e}", [P, C * 4], BF16) for e in range(E)]
        g_codes = [tile(f"g_codes{e}", [P, C], U32) for e in range(E)]
        g_scales = [tile(f"g_scales{e}", [P, C], U8) for e in range(E)]
        w_in = [tile("w_in0", [P, H * 4], BF16, tag="xg1"), tile("w_in1", [P, H * 4], BF16, tag="dy3")]
        w_codes = [tile("w_codes0", [P, H], U32, tag="gates"), tile("w_codes1", [P, H], U32)]
        w_scales = [tile(f"w_scales{e}", [P, H], U8) for e in range(E)]
        x_in = tile("x_in", [P, E * K * 4], BF16)
        x_codes = tile("x_codes", [P, E * K], U32)
        x_scales = tile("x_scales", [P, E * K], U8, tag="w_raw0")

        def weave_g(e, h, copy):
            weave(copy, g_in[e][:, h * 1024 : (h + 1) * 1024], g32[:, :, e * C + h * 256 : e * C + (h + 1) * 256])

        def weave_w(e, h):
            weave(nc.scalar.copy, w_in[e][:, h * 1024 : (h + 1) * 1024], w_raw[e][:, :, h * 256 : (h + 1) * 256])

        nc.scalar.copy(
            x_in[:].bitcast(F32).rearrange("p (e k u) -> p e k u", e=E, u=2),
            x_bank[:].rearrange("p e u k -> p e k u"),
        )
        weave_w(0, 0)
        weave_w(0, 1)
        weave_g(0, 0, nc.scalar.copy)
        weave_g(0, 1, nc.scalar.copy)
        quant(w_codes[0], w_scales[0], w_in[0], E4, 0, H)
        weave_g(1, 0, nc.vector.tensor_copy)
        quant(g_codes[0], g_scales[0], g_in[0], E5, 0, C)
        quant(x_codes, x_scales, x_in, E4, 0, E * K)
        weave_g(1, 1, nc.scalar.copy)
        weave_w(1, 0)
        weave_w(1, 1)

        da_in = [tile(f"da_in{e}", [P, H * 4], BF16) for e in range(E)]
        da_scales = [tile(f"da_scales{e}", [P, H], U8) for e in range(E)]
        dh = {}

        def product(e, b):
            cols = slice(b * P, (b + 1) * P)
            dh[e, b] = bank(f"dh{e}{b}", [P, C], 3 + b)
            nc.tensor.matmul_mx(
                dh[e, b][:], w_codes[e][:, cols].bitcast(E4), w_scales[e][:, cols], g_codes[e][:].bitcast(E5), g_scales[e][:],
                start=True, stop=True,
            )

        def turn(e, blocks, number):
            turned = bank(f"turned{e}{blocks[0]}", [P, len(blocks), 2, P], number)
            for j, b in enumerate(blocks):
                da = tile(f"da{e}{b}", [P, C], BF16)
                nc.vector.scalar_tensor_tensor(da[:], a_sb[e][b][:], 0.0, dh[e, b][:], ALU.max, ALU.mult)
                words = da[:].bitcast(F32)
                for u in range(2):
                    nc.tensor.transpose(turned[:, j, u, :], words[:, u : C // 2 : 2], ident[:])
            cols = slice(4 * P * blocks[0], 4 * P * (blocks[-1] + 1))
            nc.scalar.copy(
                da_in[e][:, cols].bitcast(F32).rearrange("p (j i u) -> p j i u", j=len(blocks), u=2),
                turned[:].rearrange("p j u i -> p j i u"),
            )

        for b in range(4):
            product(0, b)
        quant(g_codes[1], g_scales[1], g_in[1], E5, 0, C)
        turn(0, [0, 1], 0)
        quant(w_codes[1], w_scales[1], w_in[1], E4, 0, H // 2)
        product(1, 0)
        product(1, 1)
        turn(0, [2, 3], 1)
        quant(w_codes[1], w_scales[1], w_in[1], E4, H // 2, H // 2)
        product(1, 2)
        product(1, 3)
        turn(1, [0, 1], 0)
        turn(1, [2], 1)
        turn(1, [3], 2)

        da_codes = [tile("da_codes0", [P, H], U32, tag="a13"), tile("da_codes1", [P, H], U32)]

        def finish(e, pieces, number):
            acc = bank(f"acc{e}", [P, H], number)
            kc = slice(e * K, (e + 1) * K)
            nc.tensor.matmul_mx(
                acc[:], x_codes[:, kc].bitcast(E4), x_scales[:, kc], da_codes[e][:].bitcast(E5), da_scales[e][:],
                start=True, stop=True,
            )
            width = H // pieces
            for s in range(pieces):
                cols = slice(s * width, (s + 1) * width)
                res = tile(f"res{e}{s}", [P, width], F32)
                nc.scalar.activation(res[:], acc[:, cols], COPY, scale=2.0)
                nc.sync.dma_start(out[e][:, cols], res[:])

        quant(da_codes[0], da_scales[0], da_in[0], E5, 0, H)
        finish(0, 1, 7)
        quant(da_codes[1], da_scales[1], da_in[1], E5, 0, 2 * P)
        quant(da_codes[1], da_scales[1], da_in[1], E5, 2 * P, P)
        quant(da_codes[1], da_scales[1], da_in[1], E5, 3 * P, P)
        finish(1, 2, 3)
